import numpy as np
import ml_dtypes


def mxq(x, axis, fmt="e4m3"):
    dtype, down = {"e4m3": (ml_dtypes.float8_e4m3fn, 7), "e5m2": (ml_dtypes.float8_e5m2, 14)}[fmt]
    v = np.moveaxis(np.asarray(x, np.float32).astype(ml_dtypes.bfloat16).astype(np.float64), axis, -1)
    blocks = v.reshape(v.shape[:-1] + (-1, 32))
    amax = np.abs(blocks).max(-1, keepdims=True)
    byte = np.maximum(np.where(amax > 0, np.frexp(amax)[1] - 1 + 127, 0) - down, 1)
    scale = np.exp2(byte - 127.0)
    codes = (blocks / scale).astype(np.float32).astype(dtype).astype(np.float64)
    return np.moveaxis((codes * scale).reshape(v.shape), -1, axis)


WIDE = False


def mx_kscale(k):
    if not WIDE:
        return np.ones(k)
    levels = np.array([10, -10, 5, -5, 0])
    if k % 512:
        return np.exp2(np.random.permutation(np.resize(levels, k // 32))).repeat(32)
    a = np.empty((k // 512, 16))
    for p in range(k // 512):
        a[p, :8] = np.random.permutation(np.resize(levels, 8))
        for g in range(8):
            far = levels[np.abs(levels - a[p, g]) >= 10]
            a[p, g + 8] = far[np.random.randint(len(far))]
    return np.exp2(a.ravel()).repeat(32)


def f64(x):
    return np.asarray(x).astype(np.float64)


def striped(idx):
    return np.tile(np.asarray(idx).reshape(-1, 16).T, (8, 1)).astype(np.uint16)


def unstriped(offs):
    return offs[:16].T.reshape(-1).astype(np.int64)


def striped8(idx):
    return np.asarray(idx).reshape(8, -1, 16).transpose(0, 2, 1).reshape(128, -1).astype(np.uint16)


def unstriped8(offs):
    return offs.reshape(8, 16, -1).transpose(0, 2, 1).reshape(8, -1).astype(np.int64)


def pick8(x, idx, run):
    r = np.arange(len(x))
    return x[r[:, None], idx[r % (8 * run) // run]]


E2M1 = np.array([0.0, 0.5, 1.0, 1.5, 2.0, 3.0, 4.0, 6.0, -0.0, -0.5, -1.0, -1.5, -2.0, -3.0, -4.0, -6.0])


def pack_weight(w, fmt):
    k, n = w.shape
    w = f64(np.asarray(w, np.float32).astype(ml_dtypes.bfloat16)).reshape(k // 32, 32, n)
    amax = np.abs(w).max(1)
    if fmt == "e4m3":
        byte = np.frexp(amax)[1] - 1 + 127 - 7
    else:
        mant, ex = np.frexp(amax / 6.0)
        byte = np.where(mant > 0.5, ex, ex - 1) + 127
    byte = np.clip(np.where(amax > 0, byte, 1), 1, 254)
    scaled = (w * np.exp2(127.0 - byte)[:, None, :]).reshape(k, n).astype(np.float32)
    by_word = np.ascontiguousarray(scaled.reshape(k // 512, 128, 4, n).transpose(0, 1, 3, 2))
    if fmt == "e4m3":
        words = by_word.astype(ml_dtypes.float8_e4m3fn).view(np.uint8)
    else:
        c = by_word.astype(ml_dtypes.float4_e2m1fn).view(np.uint8) & 0xF
        words = (c[..., 0::2] | (c[..., 1::2] << 4)).reshape(k // 512, 128, 2 * n)
    return np.ascontiguousarray(words), np.ascontiguousarray(byte.astype(np.uint8).reshape(k // 512, 16, n))


def unpack_weight(words, scales, fmt):
    g, _, n = scales.shape
    words = np.ascontiguousarray(words).reshape(g, 128, n, -1)
    if fmt == "e4m3":
        vals = words.view(ml_dtypes.float8_e4m3fn).astype(np.float64)
    else:
        nib = np.empty((g, 128, n, 4), np.uint8)
        nib[..., 0::2] = words & 0xF
        nib[..., 1::2] = words >> 4
        vals = E2M1[nib]
    vals = vals * np.repeat(np.exp2(scales.astype(np.float64) - 127.0), 8, axis=1)[..., None]
    return vals.transpose(0, 1, 3, 2).reshape(g * 512, n)


def bf(x):
    return np.asarray(x, np.float32).astype(ml_dtypes.bfloat16)


def planes(Y):
    r, m = Y.shape
    b = f64(bf(Y)).reshape(r // 32, 32, m)
    amax = np.abs(b).max(1)
    byte = np.clip(np.where(amax > 0, np.frexp(amax)[1] - 1 + 127 - 7, 1), 1, 254)
    codes = (b * np.exp2(127.0 - byte)[:, None, :]).reshape(r, m).astype(np.float32).astype(ml_dtypes.float8_e4m3fn).view(np.uint8)
    words = codes.reshape(r // 512, 128, 4, m).transpose(0, 1, 3, 2)
    return np.ascontiguousarray(words), np.ascontiguousarray(byte.astype(np.uint8).reshape(r // 512, 16, m))


K, T, J, I, L, N = 1024, 2048, 512, 512, 512, 512


def setup_inputs():
    n = np.random.standard_normal
    idx = np.random.permutation(T)[:J]
    idx2 = np.stack([np.random.randint(0, J, I) for _ in range(8)])
    fk = mx_kscale(K)
    fl = mx_kscale(L)
    xtp = pack_weight(n((K, T)) / fk[:, None], "e2m1")
    wp = pack_weight(n((K, N)) * 1 / np.sqrt(K) * fk[:, None], "e4m3")
    wip = pack_weight(n((L, N)) * 1 / np.sqrt(L) * fl[:, None], "e2m1")
    return {
        "xt_words": xtp[0],
        "xt_scales": xtp[1],
        "w_words": wp[0],
        "w_scales": wp[1],
        "xi": (n((L, I)) / fl[:, None]).astype(np.float32),
        "wi_words": wip[0],
        "wi_scales": wip[1],
        "offs": striped(idx),
        "offs2": striped8(idx2),
    }


def reference(xt_words, xt_scales, w_words, w_scales, xi, wi_words, wi_scales, offs, offs2):
    idx = unstriped(offs)
    idx2 = unstriped8(offs2)
    xtu = unpack_weight(xt_words, xt_scales, "e2m1")
    wu = unpack_weight(w_words, w_scales, "e4m3")
    wiu = unpack_weight(wi_words, wi_scales, "e2m1")
    xtidxg = xtu[:, idx]
    z = wu.T @ xtidxg
    xiq = mxq(f64(xi), 0, "e4m3")
    q = wiu.T @ xiq
    y = pick8(z, idx2, 64) * q
    words, scales = planes(y)
    return y, words, scales

@@ -1,0 +1,179 @@
+from contextlib import ExitStack
+
+import concourse.mybir as mybir
+
+K, T, J, I, L, N = 1024, 2048, 512, 512, 512, 512
+FLOPS = 2 * K * N * J + 2 * L * N * I
+
+F32 = mybir.dt.float32
+BF16 = mybir.dt.bfloat16
+I32 = mybir.dt.int32
+U16 = mybir.dt.uint16
+U8 = mybir.dt.uint8
+FP8X4 = mybir.dt.float8_e4m3fn_x4
+FP4X4 = mybir.dt.float4_e2m1fn_x4
+MULT = mybir.AluOpType.mult
+
+P = 128
+HALF = I // 2
+CHUNKS = ((0, 256), (256, 384), (384, 512))
+
+
+def deal(nc, dst, src, run):
+    nc.vector.tensor_copy(
+        out=dst.rearrange("p z (t c i) -> p z c t i", t=4, i=run),
+        in_=src.rearrange("p z (c i t) -> p z c t i", t=4, i=run),
+    )
+
+
+def weave(engine_copy, dst, src):
+    engine_copy(
+        out=dst.rearrange("p (c i t) -> p c t i", t=4, i=4),
+        in_=src.rearrange("p t (c i) -> p c t i", i=4),
+    )
+
+
+def tile_list_shared_list_then_heads_pl_kernel(
+    tc, xt_words, xt_scales, w_words, w_scales, xi, wi_words, wi_scales, offs, offs2, out_0, out_1, out_2
+):
+    nc = tc.nc
+    with ExitStack() as ctx:
+        sb = ctx.enter_context(tc.tile_pool(name="sb", bufs=1))
+        ps = ctx.enter_context(tc.psum_pool(name="ps", bufs=1))
+
+        def tile(shape, dtype, name):
+            return sb.tile(shape, dtype, name=name, align_bytes=64)
+
+        slots = sb.tile([P, J // 16], U16, name="slots")
+        picks = sb.tile([P, I // 16], U16, name="picks")
+        xw = [tile([P, T], U16, "xw%d" % z) for z in range(2)]
+        xs = tile([P, T], U8, "xs")
+        ww = tile([P, 2, N], I32, "ww")
+        ws = tile([P, 2, N], U8, "ws")
+        wiw = tile([P, 1, N], U16, "wiw")
+        wis = tile([P, 1, N], U8, "wis")
+        xif = [tile([P, 4, HALF], F32, "xif%d" % h) for h in range(2)]
+        xs1 = tile([P, J], U8, "xs1")
+
+        nc.vector.memset(xs[:].bitcast(I32), 0)
+        nc.vector.memset(wis[:].rearrange("p z n -> p (z n)").bitcast(I32), 0)
+        nc.vector.memset(ws[:].rearrange("p z n -> p (z n)").bitcast(I32), 0)
+        nc.vector.memset(xs1[:].bitcast(I32), 0)
+
+        xi_rows = xi.rearrange("(p t) i -> p t i", t=4)
+        for q in range(4):
+            nc.scalar.dma_start(
+                out=xs[32 * q : 32 * q + 8, :].bitcast(I32), in_=xt_scales[:, 4 * q : 4 * q + 4, :].bitcast(I32)
+            )
+        for q in range(4):
+            nc.scalar.dma_start(
+                out=wis[32 * q : 32 * q + 4, 0, :].bitcast(I32), in_=wi_scales[0, 4 * q : 4 * q + 4, :].bitcast(I32)
+            )
+        nc.sync.dma_start(slots[:], offs)
+        nc.sync.dma_start(out=xw[0][:].bitcast(I32), in_=xt_words[0].bitcast(I32))
+        nc.sync.dma_start(out=xif[0][:], in_=xi_rows[:, :, 0:HALF])
+        nc.sync.dma_start(out=xw[1][:].bitcast(I32), in_=xt_words[1].bitcast(I32))
+        nc.sync.dma_start(out=wiw[:, 0, :].bitcast(I32), in_=wi_words[0].bitcast(I32))
+        nc.sync.dma_start(out=ww[:], in_=w_words.rearrange("z p n r -> p z (n r)").bitcast(I32))
+        for q in range(4):
+            nc.sync.dma_start(
+                out=ws[32 * q : 32 * q + 4, :, :].bitcast(I32),
+                in_=w_scales[:, 4 * q : 4 * q + 4, :].rearrange("z r n -> r z n").bitcast(I32),
+            )
+        nc.sync.dma_start(out=xif[1][:], in_=xi_rows[:, :, HALF:I])
+        nc.sync.dma_start(picks[:], offs2)
+
+        xg = [tile([P, J], U16, "xg%d" % z) for z in range(2)]
+        xs0 = tile([P, J], U8, "xs0")
+        wwd = tile([P, 2, N], I32, "wwd")
+        wsd = tile([P, 2, N], U8, "wsd")
+        wiwd = tile([P, 1, N], U16, "wiwd")
+        wisd = tile([P, 1, N], U8, "wisd")
+        xib = [tile([P, 4 * HALF], BF16, "xib%d" % h) for h in range(2)]
+        xq = [tile([P, HALF], I32, "xq%d" % h) for h in range(2)]
+        xqs = [tile([P, HALF], U8, "xqs%d" % h) for h in range(2)]
+        zp = [ps.tile([P, J], F32, name="zp%d" % t) for t in range(4)]
+        qp = [[ps.tile([P, 2, HALF], F32, name="qp%d%d" % (h, u)) for u in range(2)] for h in range(2)]
+        zs = [tile([P, J], F32, "zs%d" % t) for t in range(4)]
+        qs = [[tile([P, 2, HALF], F32, "qs%d%d" % (h, u)) for u in range(2)] for h in range(2)]
+        xplanes = (xs0, xs1)
+
+        def z_pass(t, z):
+            cols = slice(P * t, P * (t + 1))
+            nc.tensor.matmul_mx(
+                out=zp[t][:],
+                lhsT=wwd[:, z, cols].bitcast(FP8X4),
+                lhsT_scale=wsd[:, z, cols],
+                rhs=xg[z][:].bitcast(FP4X4),
+                rhs_scale=xplanes[z][:],
+                start=(z == 0),
+                stop=(z == 1),
+            )
+
+        def q_half(h):
+            nc.vector.quantize_mx(out=xq[h][:].bitcast(FP8X4), scales=xqs[h][:], in_=xib[h][:])
+            for t in range(4):
+                cols = slice(P * t, P * (t + 1))
+                nc.tensor.matmul_mx(
+                    out=qp[h][t // 2][:, t % 2, :],
+                    lhsT=wiwd[:, 0, cols].bitcast(FP4X4),
+                    lhsT_scale=wisd[:, 0, cols],
+                    rhs=xq[h][:].bitcast(FP8X4),
+                    rhs_scale=xqs[h][:],
+                    start=True,
+                    stop=True,
+                )
+            for u in range(2):
+                nc.scalar.copy(out=qs[h][u][:], in_=qp[h][u][:])
+
+        nc.vector.tensor_copy(out=xg[0][:], in_=xw[0][:].indirect(slots[:]))
+        nc.vector.tensor_copy(out=xs0[:], in_=xs[:].indirect(slots[:]))
+        nc.scalar.dma_start(out=xs1[0:112, :].bitcast(I32), in_=xs0[4:116, :].bitcast(I32))
+        nc.vector.tensor_copy(out=xg[1][:], in_=xw[1][:].indirect(slots[:]))
+        weave(nc.scalar.copy, xib[0][:], xif[0][:])
+        deal(nc, wiwd[:], wiw[:], 8)
+        deal(nc, wisd[:], wis[:], 16)
+        q_half(0)
+        deal(nc, wwd[:], ww[:], 4)
+        deal(nc, wsd[:], ws[:], 16)
+        for t in range(4):
+            z_pass(t, 0)
+            z_pass(t, 1)
+            nc.scalar.copy(out=zs[t][:], in_=zp[t][:])
+        weave(nc.vector.tensor_copy, xib[1][:], xif[1][:])
+        q_half(1)
+
+        yq = tile([P, I], I32, "yq")
+        yqs = tile([P, I], U8, "yqs")
+        y_rows = out_0.rearrange("(p t) i -> p t i", t=4)
+        code_rows = out_1[0].rearrange("p c r -> p (c r)").bitcast(I32)
+        ybs = []
+
+        def finish(c):
+            lo, hi = CHUNKS[c]
+            nc.vector.quantize_mx(out=yq[:, lo:hi].bitcast(FP8X4), scales=yqs[:, lo:hi], in_=ybs[c][:])
+            nc.sync.dma_start(out=code_rows[:, lo:hi], in_=yq[:, lo:hi])
+
+        for c, (lo, hi) in enumerate(CHUNKS):
+            y = tile([P, 4, hi - lo], F32, "y%d" % c)
+            yb = tile([P, 4 * (hi - lo)], BF16, "yb%d" % c)
+            ybs.append(yb)
+            h = lo // HALF
+            for t in range(4):
+                nc.vector.tensor_tensor(
+                    y[:, t, :],
+                    zs[t][:].indirect(picks[:, lo // 16 : hi // 16]),
+                    qs[h][t // 2][:, t % 2, lo - h * HALF : hi - h * HALF],
+                    MULT,
+                )
+            nc.sync.dma_start(out=y_rows[:, :, lo:hi], in_=y[:])
+            last = c == len(CHUNKS) - 1
+            weave(nc.vector.tensor_copy if last else nc.scalar.copy, yb[:], y[:])
+            if c > 0:
+                finish(c - 1)
+        finish(len(CHUNKS) - 1)
+        for q in range(4):
+            queue = nc.scalar if q % 2 else nc.sync
+            queue.dma_start(
+                out=out_2[0, 4 * q : 4 * q + 4, :].bitcast(I32), in_=yqs[32 * q : 32 * q + 4, :].bitcast(I32)
+            )

@@ -26,6 +26,13 @@ def deal(nc, dst, src, run):
     )
 
 
+def deal_slices(nc, dst, src, run, t0, t1):
+    nc.vector.tensor_copy(
+        out=dst.rearrange("p z (t c i) -> p z c t i", t=4, i=run)[:, :, :, t0:t1, :],
+        in_=src.rearrange("p z (c i t) -> p z c t i", t=4, i=run)[:, :, :, t0:t1, :],
+    )
+
+
 def weave(engine_copy, dst, src):
     engine_copy(
         out=dst.rearrange("p (c i t) -> p c t i", t=4, i=4),
@@ -56,7 +63,7 @@ def tile_list_shared_list_then_heads_pl_kernel(
         xs1 = tile([P, J], U8, "xs1")
 
         nc.vector.memset(xs[:].bitcast(I32), 0)
-        nc.vector.memset(wis[:].rearrange("p z n -> p (z n)").bitcast(I32), 0)
+        nc.gpsimd.memset(wis[:].rearrange("p z n -> p (z n)").bitcast(I32), 0)
         nc.vector.memset(ws[:].rearrange("p z n -> p (z n)").bitcast(I32), 0)
         nc.vector.memset(xs1[:].bitcast(I32), 0)
 
@@ -66,14 +73,14 @@ def tile_list_shared_list_then_heads_pl_kernel(
                 out=xs[32 * q : 32 * q + 8, :].bitcast(I32), in_=xt_scales[:, 4 * q : 4 * q + 4, :].bitcast(I32)
             )
         for q in range(4):
-            nc.scalar.dma_start(
+            nc.gpsimd.dma_start(
                 out=wis[32 * q : 32 * q + 4, 0, :].bitcast(I32), in_=wi_scales[0, 4 * q : 4 * q + 4, :].bitcast(I32)
             )
         nc.sync.dma_start(slots[:], offs)
         nc.sync.dma_start(out=xw[0][:].bitcast(I32), in_=xt_words[0].bitcast(I32))
         nc.sync.dma_start(out=xif[0][:], in_=xi_rows[:, :, 0:HALF])
-        nc.sync.dma_start(out=xw[1][:].bitcast(I32), in_=xt_words[1].bitcast(I32))
         nc.sync.dma_start(out=wiw[:, 0, :].bitcast(I32), in_=wi_words[0].bitcast(I32))
+        nc.sync.dma_start(out=xw[1][:].bitcast(I32), in_=xt_words[1].bitcast(I32))
         nc.sync.dma_start(out=ww[:], in_=w_words.rearrange("z p n r -> p z (n r)").bitcast(I32))
         for q in range(4):
             nc.sync.dma_start(
@@ -88,7 +95,6 @@ def tile_list_shared_list_then_heads_pl_kernel(
         wwd = tile([P, 2, N], I32, "wwd")
         wsd = tile([P, 2, N], U8, "wsd")
         wiwd = tile([P, 1, N], U16, "wiwd")
-        wisd = tile([P, 1, N], U8, "wisd")
         xib = [tile([P, 4 * HALF], BF16, "xib%d" % h) for h in range(2)]
         xq = [tile([P, HALF], I32, "xq%d" % h) for h in range(2)]
         xqs = [tile([P, HALF], U8, "xqs%d" % h) for h in range(2)]
@@ -110,8 +116,10 @@ def tile_list_shared_list_then_heads_pl_kernel(
                 stop=(z == 1),
             )
 
-        def q_half(h):
+        def quantise(h):
             nc.vector.quantize_mx(out=xq[h][:].bitcast(FP8X4), scales=xqs[h][:], in_=xib[h][:])
+
+        def q_half(h, wisd):
             for t in range(4):
                 cols = slice(P * t, P * (t + 1))
                 nc.tensor.matmul_mx(
@@ -128,20 +136,24 @@ def tile_list_shared_list_then_heads_pl_kernel(
 
         nc.vector.tensor_copy(out=xg[0][:], in_=xw[0][:].indirect(slots[:]))
         nc.vector.tensor_copy(out=xs0[:], in_=xs[:].indirect(slots[:]))
-        nc.scalar.dma_start(out=xs1[0:112, :].bitcast(I32), in_=xs0[4:116, :].bitcast(I32))
-        nc.vector.tensor_copy(out=xg[1][:], in_=xw[1][:].indirect(slots[:]))
         weave(nc.scalar.copy, xib[0][:], xif[0][:])
+        nc.scalar.dma_start(out=xs1[0:112, :].bitcast(I32), in_=xs0[4:116, :].bitcast(I32))
         deal(nc, wiwd[:], wiw[:], 8)
+        quantise(0)
+        wisd = tile([P, 1, N], U8, "xib0")
         deal(nc, wisd[:], wis[:], 16)
-        q_half(0)
+        q_half(0, wisd)
+        nc.vector.tensor_copy(out=xg[1][:], in_=xw[1][:].indirect(slots[:]))
         deal(nc, wwd[:], ww[:], 4)
-        deal(nc, wsd[:], ws[:], 16)
+        deal_slices(nc, wsd[:], ws[:], 16, 0, 1)
+        deal_slices(nc, wsd[:], ws[:], 16, 1, 4)
         for t in range(4):
             z_pass(t, 0)
             z_pass(t, 1)
             nc.scalar.copy(out=zs[t][:], in_=zp[t][:])
         weave(nc.vector.tensor_copy, xib[1][:], xif[1][:])
-        q_half(1)
+        quantise(1)
+        q_half(1, wisd)
 
         yq = tile([P, I], I32, "yq")
         yqs = tile([P, I], U8, "yqs")

@@ -21,15 +21,8 @@ CHUNKS = ((0, 256), (256, 384), (384, 512))
 
 def deal(nc, dst, src, run):
     nc.vector.tensor_copy(
-        out=dst.rearrange("p z (t c i) -> p z c t i", t=4, i=run),
-        in_=src.rearrange("p z (c i t) -> p z c t i", t=4, i=run),
-    )
-
-
-def deal_slices(nc, dst, src, run, t0, t1):
-    nc.vector.tensor_copy(
-        out=dst.rearrange("p z (t c i) -> p z c t i", t=4, i=run)[:, :, :, t0:t1, :],
-        in_=src.rearrange("p z (c i t) -> p z c t i", t=4, i=run)[:, :, :, t0:t1, :],
+        out=dst.rearrange("p z (t c i) -> p c z t i", t=4, i=run),
+        in_=src.rearrange("p z (c i t) -> p c z t i", t=4, i=run),
     )
 
 
@@ -56,77 +49,79 @@ def tile_list_shared_list_then_heads_pl_kernel(
         xw = [tile([P, T], U16, "xw%d" % z) for z in range(2)]
         xs = tile([P, T], U8, "xs")
         ww = tile([P, 2, N], I32, "ww")
-        ws = tile([P, 2, N], U8, "ws")
         wiw = tile([P, 1, N], U16, "wiw")
+        ws = tile([P, 2, N], U8, "ws")
         wis = tile([P, 1, N], U8, "wis")
         xif = [tile([P, 4, HALF], F32, "xif%d" % h) for h in range(2)]
         xs1 = tile([P, J], U8, "xs1")
 
+        def words(ap):
+            return ap.rearrange("p z n -> p (z n)").bitcast(I32)
+
         nc.vector.memset(xs[:].bitcast(I32), 0)
-        nc.gpsimd.memset(wis[:].rearrange("p z n -> p (z n)").bitcast(I32), 0)
-        nc.vector.memset(ws[:].rearrange("p z n -> p (z n)").bitcast(I32), 0)
-        nc.vector.memset(xs1[:].bitcast(I32), 0)
+        nc.gpsimd.memset(words(wis[:]), 0)
+        nc.gpsimd.memset(words(ws[:]), 0)
+        nc.gpsimd.memset(xs1[:].bitcast(I32), 0)
 
         xi_rows = xi.rearrange("(p t) i -> p t i", t=4)
-        for q in range(4):
-            nc.scalar.dma_start(
-                out=xs[32 * q : 32 * q + 8, :].bitcast(I32), in_=xt_scales[:, 4 * q : 4 * q + 4, :].bitcast(I32)
-            )
-        for q in range(4):
-            nc.gpsimd.dma_start(
-                out=wis[32 * q : 32 * q + 4, 0, :].bitcast(I32), in_=wi_scales[0, 4 * q : 4 * q + 4, :].bitcast(I32)
-            )
+        xs_rows = xt_scales.rearrange("z (q r) c -> r q z c", r=4).bitcast(I32)
+        ws_rows = w_scales.rearrange("z (q r) n -> r q z n", r=4).bitcast(I32)
+        wis_rows = wi_scales.rearrange("z (q r) n -> r q z n", r=4).bitcast(I32)
         nc.sync.dma_start(slots[:], offs)
         nc.sync.dma_start(out=xw[0][:].bitcast(I32), in_=xt_words[0].bitcast(I32))
-        nc.sync.dma_start(out=xif[0][:], in_=xi_rows[:, :, 0:HALF])
+        for r in range(4):
+            nc.sync.dma_start(out=xs[r:P:16, :].bitcast(I32), in_=xs_rows[r])
         nc.sync.dma_start(out=wiw[:, 0, :].bitcast(I32), in_=wi_words[0].bitcast(I32))
-        nc.sync.dma_start(out=xw[1][:].bitcast(I32), in_=xt_words[1].bitcast(I32))
+        nc.sync.dma_start(out=wis[0:P:32, :, :].bitcast(I32), in_=wis_rows[0])
+        nc.sync.dma_start(out=xif[0][:], in_=xi_rows[:, :, 0:HALF])
+        for r in range(1, 4):
+            nc.sync.dma_start(out=wis[r:P:32, :, :].bitcast(I32), in_=wis_rows[r])
+        for r in range(3):
+            nc.sync.dma_start(out=ws[r:P:32, :, :].bitcast(I32), in_=ws_rows[r])
         nc.sync.dma_start(out=ww[:], in_=w_words.rearrange("z p n r -> p z (n r)").bitcast(I32))
-        for q in range(4):
-            nc.sync.dma_start(
-                out=ws[32 * q : 32 * q + 4, :, :].bitcast(I32),
-                in_=w_scales[:, 4 * q : 4 * q + 4, :].rearrange("z r n -> r z n").bitcast(I32),
-            )
-        nc.sync.dma_start(out=xif[1][:], in_=xi_rows[:, :, HALF:I])
-        nc.sync.dma_start(picks[:], offs2)
+        nc.sync.dma_start(out=ws[3:P:32, :, :].bitcast(I32), in_=ws_rows[3])
+        nc.sync.dma_start(out=xw[1][:].bitcast(I32), in_=xt_words[1].bitcast(I32))
 
         xg = [tile([P, J], U16, "xg%d" % z) for z in range(2)]
         xs0 = tile([P, J], U8, "xs0")
-        wwd = tile([P, 2, N], I32, "wwd")
         wsd = tile([P, 2, N], U8, "wsd")
+        wisd = tile([P, 1, N], U8, "wisd")
+        xq = [tile([P, HALF], I32, "xq%d" % h) for h in range(2)]
+        wwd = [tile([P, 2, 2 * P], I32, "wwd0")]
         wiwd = tile([P, 1, N], U16, "wiwd")
         xib = [tile([P, 4 * HALF], BF16, "xib%d" % h) for h in range(2)]
-        xq = [tile([P, HALF], I32, "xq%d" % h) for h in range(2)]
         xqs = [tile([P, HALF], U8, "xqs%d" % h) for h in range(2)]
         zp = [ps.tile([P, J], F32, name="zp%d" % t) for t in range(4)]
         qp = [[ps.tile([P, 2, HALF], F32, name="qp%d%d" % (h, u)) for u in range(2)] for h in range(2)]
         zs = [tile([P, J], F32, "zs%d" % t) for t in range(4)]
         qs = [[tile([P, 2, HALF], F32, "qs%d%d" % (h, u)) for u in range(2)] for h in range(2)]
-        xplanes = (xs0, xs1)
 
         def z_pass(t, z):
-            cols = slice(P * t, P * (t + 1))
             nc.tensor.matmul_mx(
                 out=zp[t][:],
-                lhsT=wwd[:, z, cols].bitcast(FP8X4),
-                lhsT_scale=wsd[:, z, cols],
+                lhsT=wwd[t // 2][:, z, P * (t % 2) : P * (t % 2 + 1)].bitcast(FP8X4),
+                lhsT_scale=wsd[:, z, P * t : P * (t + 1)],
                 rhs=xg[z][:].bitcast(FP4X4),
-                rhs_scale=xplanes[z][:],
+                rhs_scale=(xs0, xs1)[z][:],
                 start=(z == 0),
                 stop=(z == 1),
             )
 
-        def quantise(h):
-            nc.vector.quantize_mx(out=xq[h][:].bitcast(FP8X4), scales=xqs[h][:], in_=xib[h][:])
+        def deal_w(u):
+            nc.vector.tensor_copy(
+                out=wwd[u][:].rearrange("p z (t c i) -> p z c t i", t=2, i=4),
+                in_=ww[:].rearrange("p z (c i t) -> p z c t i", t=4, i=4)[:, :, :, 2 * u : 2 * u + 2, :],
+            )
 
-        def q_half(h, wisd):
+        def q_half(h, xq):
+            nc.vector.quantize_mx(out=xq[:].bitcast(FP8X4), scales=xqs[h][:], in_=xib[h][:])
             for t in range(4):
                 cols = slice(P * t, P * (t + 1))
                 nc.tensor.matmul_mx(
                     out=qp[h][t // 2][:, t % 2, :],
                     lhsT=wiwd[:, 0, cols].bitcast(FP4X4),
                     lhsT_scale=wisd[:, 0, cols],
-                    rhs=xq[h][:].bitcast(FP8X4),
+                    rhs=xq[:].bitcast(FP8X4),
                     rhs_scale=xqs[h][:],
                     start=True,
                     stop=True,
@@ -136,24 +131,27 @@ def tile_list_shared_list_then_heads_pl_kernel(
 
         nc.vector.tensor_copy(out=xg[0][:], in_=xw[0][:].indirect(slots[:]))
         nc.vector.tensor_copy(out=xs0[:], in_=xs[:].indirect(slots[:]))
+        nc.sync.dma_start(out=xs1[0:112, :].bitcast(I32), in_=xs0[16:P, :].bitcast(I32))
+        nc.sync.dma_start(picks[:], offs2)
+        nc.sync.dma_start(out=xif[1][:], in_=xi_rows[:, :, HALF:I])
         weave(nc.scalar.copy, xib[0][:], xif[0][:])
-        nc.scalar.dma_start(out=xs1[0:112, :].bitcast(I32), in_=xs0[4:116, :].bitcast(I32))
         deal(nc, wiwd[:], wiw[:], 8)
-        quantise(0)
-        wisd = tile([P, 1, N], U8, "xib0")
         deal(nc, wisd[:], wis[:], 16)
-        q_half(0, wisd)
-        nc.vector.tensor_copy(out=xg[1][:], in_=xw[1][:].indirect(slots[:]))
-        deal(nc, wwd[:], ww[:], 4)
-        deal_slices(nc, wsd[:], ws[:], 16, 0, 1)
-        deal_slices(nc, wsd[:], ws[:], 16, 1, 4)
-        for t in range(4):
+        q_half(0, xq[0])
+        deal_w(0)
+        deal(nc, wsd[:], ws[:], 16)
+        for t in range(2):
             z_pass(t, 0)
+        nc.vector.tensor_copy(out=xg[1][:], in_=xw[1][:].indirect(slots[:]))
+        wwd.append(tile([P, 2, 2 * P], I32, "xw1"))
+        deal_w(1)
+        for t in range(4):
+            if t >= 2:
+                z_pass(t, 0)
             z_pass(t, 1)
             nc.scalar.copy(out=zs[t][:], in_=zp[t][:])
         weave(nc.vector.tensor_copy, xib[1][:], xif[1][:])
-        quantise(1)
-        q_half(1, wisd)
+        q_half(1, xq[1])
 
         yq = tile([P, I], I32, "yq")
         yqs = tile([P, I], U8, "yqs")
@@ -167,7 +165,7 @@ def tile_list_shared_list_then_heads_pl_kernel(
             nc.sync.dma_start(out=code_rows[:, lo:hi], in_=yq[:, lo:hi])
 
         for c, (lo, hi) in enumerate(CHUNKS):
-            y = tile([P, 4, hi - lo], F32, "y%d" % c)
+            y = tile([P, 4, hi - lo], F32, "xib1" if c == 0 else "y%d" % c)
             yb = tile([P, 4 * (hi - lo)], BF16, "yb%d" % c)
             ybs.append(yb)
             h = lo // HALF

from contextlib import ExitStack

import concourse.mybir as mybir

K, T, J, I, L, N = 1024, 2048, 512, 512, 512, 512
FLOPS = 2 * K * N * J + 2 * L * N * I

F32 = mybir.dt.float32
BF16 = mybir.dt.bfloat16
I32 = mybir.dt.int32
U16 = mybir.dt.uint16
U8 = mybir.dt.uint8
FP8X4 = mybir.dt.float8_e4m3fn_x4
FP4X4 = mybir.dt.float4_e2m1fn_x4
MULT = mybir.AluOpType.mult

P = 128
HALF = I // 2
CHUNKS = ((0, 256), (256, 384), (384, 512))


def deal(nc, dst, src, run):
    nc.vector.tensor_copy(
        out=dst.rearrange("p z (t c i) -> p c z t i", t=4, i=run),
        in_=src.rearrange("p z (c i t) -> p c z t i", t=4, i=run),
    )


def weave(engine_copy, dst, src):
    engine_copy(
        out=dst.rearrange("p (c i t) -> p c t i", t=4, i=4),
        in_=src.rearrange("p t (c i) -> p c t i", i=4),
    )


def tile_list_shared_list_then_heads_pl_kernel(
    tc, xt_words, xt_scales, w_words, w_scales, xi, wi_words, wi_scales, offs, offs2, out_0, out_1, out_2
):
    nc = tc.nc
    with ExitStack() as ctx:
        sb = ctx.enter_context(tc.tile_pool(name="sb", bufs=1))
        ps = ctx.enter_context(tc.psum_pool(name="ps", bufs=1))

        def tile(shape, dtype, name):
            return sb.tile(shape, dtype, name=name, align_bytes=64)

        slots = sb.tile([P, J // 16], U16, name="slots")
        picks = sb.tile([P, I // 16], U16, name="picks")
        xw = [tile([P, T], U16, "xw%d" % z) for z in range(2)]
        xs = tile([P, T], U8, "xs")
        ww = tile([P, 2, N], I32, "ww")
        wiw = tile([P, 1, N], U16, "wiw")
        ws = tile([P, 2, N], U8, "ws")
        wis = tile([P, 1, N], U8, "wis")
        xif = [tile([P, 4, HALF], F32, "xif%d" % h) for h in range(2)]
        xs1 = tile([P, J], U8, "xs1")

        def words(ap):
            return ap.rearrange("p z n -> p (z n)").bitcast(I32)

        nc.vector.memset(xs[:].bitcast(I32), 0)
        nc.gpsimd.memset(words(wis[:]), 0)
        nc.gpsimd.memset(words(ws[:]), 0)
        nc.gpsimd.memset(xs1[:].bitcast(I32), 0)

        xi_rows = xi.rearrange("(p t) i -> p t i", t=4)
        xs_rows = xt_scales.rearrange("z (q r) c -> r q z c", r=4).bitcast(I32)
        ws_rows = w_scales.rearrange("z (q r) n -> r q z n", r=4).bitcast(I32)
        wis_rows = wi_scales.rearrange("z (q r) n -> r q z n", r=4).bitcast(I32)
        nc.sync.dma_start(slots[:], offs)
        nc.sync.dma_start(out=xw[0][:].bitcast(I32), in_=xt_words[0].bitcast(I32))
        for r in range(4):
            nc.sync.dma_start(out=xs[r:P:16, :].bitcast(I32), in_=xs_rows[r])
        nc.sync.dma_start(out=wiw[:, 0, :].bitcast(I32), in_=wi_words[0].bitcast(I32))
        nc.sync.dma_start(out=wis[0:P:32, :, :].bitcast(I32), in_=wis_rows[0])
        nc.sync.dma_start(out=xif[0][:], in_=xi_rows[:, :, 0:HALF])
        for r in range(1, 4):
            nc.sync.dma_start(out=wis[r:P:32, :, :].bitcast(I32), in_=wis_rows[r])
        for r in range(3):
            nc.sync.dma_start(out=ws[r:P:32, :, :].bitcast(I32), in_=ws_rows[r])
        nc.sync.dma_start(out=ww[:], in_=w_words.rearrange("z p n r -> p z (n r)").bitcast(I32))
        nc.sync.dma_start(out=ws[3:P:32, :, :].bitcast(I32), in_=ws_rows[3])
        nc.sync.dma_start(out=xw[1][:].bitcast(I32), in_=xt_words[1].bitcast(I32))

        xg = [tile([P, J], U16, "xg%d" % z) for z in range(2)]
        xs0 = tile([P, J], U8, "xs0")
        wsd = tile([P, 2, N], U8, "wsd")
        wisd = tile([P, 1, N], U8, "wisd")
        xq = [tile([P, HALF], I32, "xq%d" % h) for h in range(2)]
        wwd = [tile([P, 2, 2 * P], I32, "wwd0")]
        wiwd = tile([P, 1, N], U16, "wiwd")
        xib = [tile([P, 4 * HALF], BF16, "xib%d" % h) for h in range(2)]
        xqs = [tile([P, HALF], U8, "xqs%d" % h) for h in range(2)]
        zp = [ps.tile([P, J], F32, name="zp%d" % t) for t in range(4)]
        qp = [[ps.tile([P, 2, HALF], F32, name="qp%d%d" % (h, u)) for u in range(2)] for h in range(2)]
        zs = [tile([P, J], F32, "zs%d" % t) for t in range(4)]
        qs = [[tile([P, 2, HALF], F32, "qs%d%d" % (h, u)) for u in range(2)] for h in range(2)]

        def z_pass(t, z):
            nc.tensor.matmul_mx(
                out=zp[t][:],
                lhsT=wwd[t // 2][:, z, P * (t % 2) : P * (t % 2 + 1)].bitcast(FP8X4),
                lhsT_scale=wsd[:, z, P * t : P * (t + 1)],
                rhs=xg[z][:].bitcast(FP4X4),
                rhs_scale=(xs0, xs1)[z][:],
                start=(z == 0),
                stop=(z == 1),
            )

        def deal_w(u):
            nc.vector.tensor_copy(
                out=wwd[u][:].rearrange("p z (t c i) -> p z c t i", t=2, i=4),
                in_=ww[:].rearrange("p z (c i t) -> p z c t i", t=4, i=4)[:, :, :, 2 * u : 2 * u + 2, :],
            )

        def q_half(h, xq):
            nc.vector.quantize_mx(out=xq[:].bitcast(FP8X4), scales=xqs[h][:], in_=xib[h][:])
            for t in range(4):
                cols = slice(P * t, P * (t + 1))
                nc.tensor.matmul_mx(
                    out=qp[h][t // 2][:, t % 2, :],
                    lhsT=wiwd[:, 0, cols].bitcast(FP4X4),
                    lhsT_scale=wisd[:, 0, cols],
                    rhs=xq[:].bitcast(FP8X4),
                    rhs_scale=xqs[h][:],
                    start=True,
                    stop=True,
                )
            for u in range(2):
                nc.scalar.copy(out=qs[h][u][:], in_=qp[h][u][:])

        nc.vector.tensor_copy(out=xg[0][:], in_=xw[0][:].indirect(slots[:]))
        nc.vector.tensor_copy(out=xs0[:], in_=xs[:].indirect(slots[:]))
        nc.sync.dma_start(out=xs1[0:112, :].bitcast(I32), in_=xs0[16:P, :].bitcast(I32))
        nc.sync.dma_start(picks[:], offs2)
        nc.sync.dma_start(out=xif[1][:], in_=xi_rows[:, :, HALF:I])
        weave(nc.scalar.copy, xib[0][:], xif[0][:])
        deal(nc, wiwd[:], wiw[:], 8)
        deal(nc, wisd[:], wis[:], 16)
        q_half(0, xq[0])
        deal_w(0)
        deal(nc, wsd[:], ws[:], 16)
        for t in range(2):
            z_pass(t, 0)
        nc.vector.tensor_copy(out=xg[1][:], in_=xw[1][:].indirect(slots[:]))
        wwd.append(tile([P, 2, 2 * P], I32, "xw1"))
        deal_w(1)
        for t in range(4):
            if t >= 2:
                z_pass(t, 0)
            z_pass(t, 1)
            nc.scalar.copy(out=zs[t][:], in_=zp[t][:])
        weave(nc.vector.tensor_copy, xib[1][:], xif[1][:])
        q_half(1, xq[1])

        yq = tile([P, I], I32, "yq")
        yqs = tile([P, I], U8, "yqs")
        y_rows = out_0.rearrange("(p t) i -> p t i", t=4)
        code_rows = out_1[0].rearrange("p c r -> p (c r)").bitcast(I32)
        ybs = []

        def finish(c):
            lo, hi = CHUNKS[c]
            nc.vector.quantize_mx(out=yq[:, lo:hi].bitcast(FP8X4), scales=yqs[:, lo:hi], in_=ybs[c][:])
            nc.sync.dma_start(out=code_rows[:, lo:hi], in_=yq[:, lo:hi])

        for c, (lo, hi) in enumerate(CHUNKS):
            y = tile([P, 4, hi - lo], F32, "xib1" if c == 0 else "y%d" % c)
            yb = tile([P, 4 * (hi - lo)], BF16, "yb%d" % c)
            ybs.append(yb)
            h = lo // HALF
            for t in range(4):
                nc.vector.tensor_tensor(
                    y[:, t, :],
                    zs[t][:].indirect(picks[:, lo // 16 : hi // 16]),
                    qs[h][t // 2][:, t % 2, lo - h * HALF : hi - h * HALF],
                    MULT,
                )
            nc.sync.dma_start(out=y_rows[:, :, lo:hi], in_=y[:])
            last = c == len(CHUNKS) - 1
            weave(nc.vector.tensor_copy if last else nc.scalar.copy, yb[:], y[:])
            if c > 0:
                finish(c - 1)
        finish(len(CHUNKS) - 1)
        for q in range(4):
            queue = nc.scalar if q % 2 else nc.sync
            queue.dma_start(
                out=out_2[0, 4 * q : 4 * q + 4, :].bitcast(I32), in_=yqs[32 * q : 32 * q + 4, :].bitcast(I32)
            )
